import numpy as np
import ml_dtypes


def mxq(x, axis, fmt="e4m3"):
    dtype, down = {"e4m3": (ml_dtypes.float8_e4m3fn, 7), "e5m2": (ml_dtypes.float8_e5m2, 14)}[fmt]
    v = np.moveaxis(np.asarray(x, np.float32).astype(ml_dtypes.bfloat16).astype(np.float64), axis, -1)
    blocks = v.reshape(v.shape[:-1] + (-1, 32))
    amax = np.abs(blocks).max(-1, keepdims=True)
    byte = np.maximum(np.where(amax > 0, np.frexp(amax)[1] - 1 + 127, 0) - down, 1)
    scale = np.exp2(byte - 127.0)
    codes = (blocks / scale).astype(np.float32).astype(dtype).astype(np.float64)
    return np.moveaxis((codes * scale).reshape(v.shape), -1, axis)


WIDE = False


def mx_kscale(k):
    if not WIDE:
        return np.ones(k)
    levels = np.array([10, -10, 5, -5, 0])
    if k % 512:
        return np.exp2(np.random.permutation(np.resize(levels, k // 32))).repeat(32)
    a = np.empty((k // 512, 16))
    for p in range(k // 512):
        a[p, :8] = np.random.permutation(np.resize(levels, 8))
        for g in range(8):
            far = levels[np.abs(levels - a[p, g]) >= 10]
            a[p, g + 8] = far[np.random.randint(len(far))]
    return np.exp2(a.ravel()).repeat(32)


BF16 = ml_dtypes.bfloat16


def bf(x):
    return np.asarray(x, np.float32).astype(BF16)


def f64(x):
    return np.asarray(x).astype(np.float64)


E2M1 = np.array([0.0, 0.5, 1.0, 1.5, 2.0, 3.0, 4.0, 6.0, -0.0, -0.5, -1.0, -1.5, -2.0, -3.0, -4.0, -6.0])


def pack_weight(w, fmt):
    k, n = w.shape
    w = f64(bf(w)).reshape(k // 32, 32, n)
    amax = np.abs(w).max(1)
    if fmt == "e4m3":
        byte = np.frexp(amax)[1] - 1 + 127 - 7
    else:
        mant, ex = np.frexp(amax / 6.0)
        byte = np.where(mant > 0.5, ex, ex - 1) + 127
    byte = np.clip(np.where(amax > 0, byte, 1), 1, 254)
    scaled = (w * np.exp2(127.0 - byte)[:, None, :]).reshape(k, n).astype(np.float32)
    by_word = np.ascontiguousarray(scaled.reshape(k // 512, 128, 4, n).transpose(0, 1, 3, 2))
    if fmt == "e4m3":
        words = by_word.astype(ml_dtypes.float8_e4m3fn).view(np.uint8)
    else:
        c = by_word.astype(ml_dtypes.float4_e2m1fn).view(np.uint8) & 0xF
        words = c[..., 0::2] | (c[..., 1::2] << 4)
    return np.ascontiguousarray(words), np.ascontiguousarray(byte.astype(np.uint8).reshape(k // 512, 16, n))


def unpack_weight(words, scales, fmt):
    g, p, n, _ = words.shape
    if fmt == "e4m3":
        vals = np.ascontiguousarray(words).view(ml_dtypes.float8_e4m3fn).astype(np.float64)
    else:
        nib = np.empty((g, p, n, 4), np.uint8)
        nib[..., 0::2] = words & 0xF
        nib[..., 1::2] = words >> 4
        vals = E2M1[nib]
    vals = vals * np.repeat(np.exp2(scales.astype(np.float64) - 127.0), 8, axis=1)[..., None]
    return vals.transpose(0, 1, 3, 2).reshape(g * 512, n)
def pack4(w):
    words, scales = pack_weight(w, "e2m1")
    return words.reshape(words.shape[0], 128, -1), scales


def unpack4(words, scales):
    return unpack_weight(words.reshape(words.shape[0], 128, -1, 2), scales, "e2m1")


M, KL, KR, N = 1024, 512, 1536, 2048
BETA2 = 0.9
LOUD = 2.0


def setup_inputs():
    s, u = mx_kscale(KL), mx_kscale(KR)
    grad_loud = LOUD * np.random.standard_normal((M, KL)) * s
    grad_rest = np.random.standard_normal((M, KR)) * u
    basis_loud = np.random.standard_normal((KL, N)) / np.sqrt(KL + KR) / s[:, None]
    basis_rest = np.random.standard_normal((KR, N)) / np.sqrt(KL + KR) / u[:, None]
    words, scales = pack4(basis_rest)
    moment = 0.5 + 1.5 * np.abs(np.random.standard_normal((M, N)))
    return {"grad_loud": bf(grad_loud),
            "grad_rest": bf(grad_rest),
            "basis_loud": bf(basis_loud),
            "basis_rest_words": words,
            "basis_rest_scales": scales,
            "moment": bf(moment)}


def reference(grad_loud, grad_rest, basis_loud, basis_rest_words, basis_rest_scales, moment):
    loud = mxq(f64(grad_loud), 1, "e4m3") @ mxq(f64(basis_loud), 0, "e4m3")
    rest = mxq(f64(grad_rest), 1, "e4m3") @ unpack4(basis_rest_words, basis_rest_scales)
    r = loud + rest
    new_moment = BETA2 * f64(moment) + (1 - BETA2) * (r * r)
    step = r / np.sqrt(new_moment)
    return step, new_moment

@@ -1,0 +1,247 @@
+from contextlib import ExitStack
+
+import concourse.mybir as mybir
+from concourse.masks import make_identity
+
+M, KL, KR, N = 1024, 512, 1536, 2048
+BETA2 = 0.9
+FLOPS = 2 * M * (KL + KR) * N
+
+F32 = mybir.dt.float32
+BF16 = mybir.dt.bfloat16
+I32 = mybir.dt.int32
+U32 = mybir.dt.uint32
+U8 = mybir.dt.uint8
+E4M3X4 = mybir.dt.float8_e4m3fn_x4
+E2M1X4 = mybir.dt.float4_e2m1fn_x4
+ACT = mybir.ActivationFunctionType
+ALU = mybir.AluOpType
+
+P = 128
+TILES = M // P
+BANK = 512
+HALF = 2 * BANK
+PASSES = 4
+REST = KR // 512
+
+
+def tile_soap_rotated_step_s1_kernel(
+    tc, grad_loud, grad_rest, basis_loud, basis_rest_words, basis_rest_scales, moment, out_0, out_1
+):
+    nc = tc.nc
+    loud_rows = grad_loud.rearrange("(p r) k -> p r k", r=TILES)
+    rest_rows = grad_rest.rearrange("(p r) k -> p r k", r=TILES)
+    moment_rows = moment.rearrange("(p r) n -> p r n", r=TILES)
+    step_rows = out_0.rearrange("(p r) n -> p r n", r=TILES)
+    new_moment_rows = out_1.rearrange("(p r) n -> p r n", r=TILES)
+    basis_rows = basis_loud.rearrange("(p j) n -> p j n", j=4)
+    words_i32 = basis_rest_words.bitcast(I32).rearrange("g p w -> p g w")
+    scales_i32 = basis_rest_scales.bitcast(I32).rearrange("g (q r) w -> r q g w", r=4)
+
+    with ExitStack() as ctx:
+        keep = ctx.enter_context(tc.tile_pool(name="keep", bufs=1))
+        stage = ctx.enter_context(tc.tile_pool(name="stage", bufs=3))
+        pair = ctx.enter_context(tc.tile_pool(name="pair", bufs=2))
+        results = ctx.enter_context(tc.tile_pool(name="results", bufs=4))
+        acc_pool = ctx.enter_context(tc.psum_pool(name="acc_pool", bufs=6))
+        turn_pool = ctx.enter_context(tc.psum_pool(name="turn_pool", bufs=2))
+
+        loud = keep.tile([P, TILES, KL], BF16, name="loud", align_bytes=64)
+        rest = keep.tile([P, TILES, KR], BF16, name="rest", align_bytes=64)
+        mom = keep.tile([P, TILES, N], BF16, name="mom", align_bytes=64)
+        basis = keep.tile([P, 4, N], BF16, name="basis", align_bytes=64)
+        w_words = keep.tile([P, REST, 2 * N], U8, name="w_words", align_bytes=64)
+        w_scales = keep.tile([P, REST, N], U8, name="w_scales", align_bytes=64)
+        b_codes = keep.tile([P, N], U32, name="b_codes", align_bytes=64)
+        b_scales = keep.tile([P, N], U8, name="b_scales", align_bytes=64)
+        ident = keep.tile([P, P], F32, name="ident", align_bytes=64)
+        one = keep.tile([P, 1], F32, name="one")
+        warm = keep.tile([P, 1], F32, name="warm")
+
+        ctx.enter_context(tc.manual_schedule())
+
+        def load_basis(c0, c1):
+            nc.sync.dma_start(out=basis[:, :, c0:c1], in_=basis_rows[:, :, c0:c1])
+
+        def load_loud(r0, r1):
+            nc.sync.dma_start(out=loud[:, r0:r1, :], in_=loud_rows[:, r0:r1, :])
+
+        def load_rest(r0, r1):
+            nc.sync.dma_start(out=rest[:, r0:r1, :], in_=rest_rows[:, r0:r1, :])
+
+        def load_moment(r0, r1):
+            nc.sync.dma_start(out=mom[:, r0:r1, :], in_=moment_rows[:, r0:r1, :])
+
+        nc.gpsimd.memset(one[:], 1.0)
+        nc.scalar.activation(out=warm[:], in_=one[:], func=ACT.Abs_reciprocal_sqrt)
+        nc.vector.memset(w_scales[:].rearrange("p g n -> p (g n)").bitcast(I32), 0)
+
+        load_basis(0, HALF)
+        load_loud(0, 2)
+        load_rest(0, 2)
+        load_basis(HALF, N)
+        nc.sync.dma_start(out=w_words[:].bitcast(I32), in_=words_i32)
+        load_moment(0, 1)
+        load_moment(1, 2)
+        load_rest(2, 4)
+        load_loud(2, 8)
+        load_moment(2, 4)
+        load_rest(4, 6)
+        load_moment(4, 6)
+
+        make_identity(nc, ident[:])
+        for r in range(4):
+            nc.gpsimd.dma_start(out=w_scales[r:P:32, :, :].bitcast(I32), in_=scales_i32[r])
+
+        def interleave_basis(engine_copy, c):
+            cols = slice(c * BANK, (c + 1) * BANK)
+            b_grouped = stage.tile([P, BANK, 4], BF16, name="b_grouped", align_bytes=64)
+            engine_copy(out=b_grouped[:], in_=basis[:, :, cols].rearrange("p j n -> p n j"))
+            return b_grouped
+
+        def quantize_basis(c, b_grouped):
+            cols = slice(c * BANK, (c + 1) * BANK)
+            nc.vector.quantize_mx(
+                out=b_codes[:, cols].bitcast(E4M3X4),
+                scales=b_scales[:, cols],
+                in_=b_grouped[:].rearrange("p n j -> p (n j)"),
+            )
+
+        grouped = {}
+        codes = {}
+        scales = {}
+
+        def turn(i, b):
+            if b == 0:
+                g_grouped = pair.tile([P, PASSES * P * 4], BF16, name="g_grouped", align_bytes=64)
+                grouped[i] = g_grouped
+            turned = turn_pool.tile([P, 2, 2, P], F32, name="turned")
+            loud_words = loud[:, i, :].bitcast(F32)
+            rest_words = rest[:, i, :].bitcast(F32)
+            for s in range(2):
+                g = 2 * b + s
+                for u in range(2):
+                    if g == 0:
+                        src = loud_words[:, u:256:2]
+                    else:
+                        src = rest_words[:, 256 * (g - 1) + u : 256 * g : 2]
+                    nc.tensor.transpose(turned[:, s, u, :], src, ident[:])
+            nc.scalar.copy(
+                out=grouped[i][:, 1024 * b : 1024 * (b + 1)].bitcast(F32).rearrange("p (s r u) -> p s r u", s=2, u=2),
+                in_=turned[:].rearrange("p s u r -> p s r u"),
+            )
+
+        def quantize_tile(i):
+            g_codes = stage.tile([P, PASSES * P], U32, name="g_codes", align_bytes=64)
+            g_scales = stage.tile([P, PASSES * P], U8, name="g_scales", align_bytes=64)
+            codes[i] = g_codes
+            scales[i] = g_scales
+            nc.vector.quantize_mx(out=g_codes[:].bitcast(E4M3X4), scales=g_scales[:], in_=grouped[i][:])
+
+        acc = {}
+        sq = {}
+        rs = {}
+        nm = {}
+        st = {}
+
+        def multiply(h):
+            i = h // 2
+            acc[h] = []
+            for b in range(2):
+                n0 = (h % 2) * HALF + b * BANK
+                bank = acc_pool.tile([P, BANK], F32, name="bank")
+                acc[h].append(bank)
+                for g in range(PASSES):
+                    k_cols = slice(g * P, (g + 1) * P)
+                    if g == 0:
+                        rhs = b_codes[:, n0 : n0 + BANK].bitcast(E4M3X4)
+                        rhs_scale = b_scales[:, n0 : n0 + BANK]
+                    else:
+                        rhs = w_words[:, g - 1, 2 * n0 : 2 * (n0 + BANK)].bitcast(E2M1X4)
+                        rhs_scale = w_scales[:, g - 1, n0 : n0 + BANK]
+                    nc.tensor.matmul_mx(
+                        out=bank[:],
+                        lhsT=codes[i][:, k_cols].bitcast(E4M3X4),
+                        lhsT_scale=scales[i][:, k_cols],
+                        rhs=rhs,
+                        rhs_scale=rhs_scale,
+                        start=(g == 0),
+                        stop=(g == PASSES - 1),
+                    )
+
+        def square(h):
+            squares = stage.tile([P, HALF], F32, name="squares")
+            sq[h] = squares
+            for b in range(2):
+                nc.scalar.activation(
+                    out=squares[:, b * BANK : (b + 1) * BANK],
+                    in_=acc[h][b][:],
+                    func=ACT.Square,
+                    scale=(1 - BETA2) ** 0.5,
+                )
+
+        def update_moment(h):
+            i = h // 2
+            if h % 2 == 0:
+                nm_tile = results.tile([P, N], F32, name="nm_tile")
+                nm[i] = nm_tile
+            cols = slice((h % 2) * HALF, (h % 2 + 1) * HALF)
+            nc.vector.scalar_tensor_tensor(
+                out=nm[i][:, cols], in0=mom[:, i, cols], scalar=BETA2, in1=sq[h][:], op0=ALU.mult, op1=ALU.add
+            )
+            if h % 2 == 1:
+                nc.sync.dma_start(out=new_moment_rows[:, i, :], in_=nm[i][:])
+
+        def root(h):
+            i = h // 2
+            cols = slice((h % 2) * HALF, (h % 2 + 1) * HALF)
+            roots = pair.tile([P, HALF], F32, name="roots")
+            rs[h] = roots
+            nc.scalar.activation(out=roots[:], in_=nm[i][:, cols], func=ACT.Abs_reciprocal_sqrt)
+
+        def normalise(h):
+            i = h // 2
+            if h % 2 == 0:
+                st_tile = results.tile([P, N], F32, name="st_tile")
+                st[i] = st_tile
+            for b in range(2):
+                n0 = (h % 2) * HALF + b * BANK
+                nc.vector.tensor_tensor(
+                    out=st[i][:, n0 : n0 + BANK], in0=acc[h][b][:], in1=rs[h][:, b * BANK : (b + 1) * BANK], op=ALU.mult
+                )
+            if h % 2 == 1:
+                nc.sync.dma_start(out=step_rows[:, i, :], in_=st[i][:])
+                if i == 0:
+                    load_rest(6, 8)
+                if i == 1:
+                    load_moment(6, 8)
+
+        b0 = interleave_basis(nc.vector.tensor_copy, 0)
+        b1 = interleave_basis(nc.scalar.copy, 1)
+        turn(0, 0)
+        turn(0, 1)
+        quantize_basis(0, b0)
+        turn(1, 0)
+        turn(1, 1)
+        quantize_basis(1, b1)
+        quantize_tile(0)
+        b2 = interleave_basis(nc.vector.tensor_copy, 2)
+        b3 = interleave_basis(nc.scalar.copy, 3)
+        quantize_tile(1)
+        quantize_basis(2, b2)
+        quantize_basis(3, b3)
+
+        for h in range(2 * TILES):
+            i = h // 2
+            multiply(h)
+            square(h)
+            update_moment(h)
+            if h > 0:
+                root(h - 1)
+                normalise(h - 1)
+            if i + 2 < TILES:
+                turn(i + 2, h % 2)
+                if h % 2 == 1:
+                    quantize_tile(i + 2)
+        root(2 * TILES - 1)
+        normalise(2 * TILES - 1)

@@ -40,16 +40,18 @@ def tile_soap_rotated_step_s1_kernel(
 
     with ExitStack() as ctx:
         keep = ctx.enter_context(tc.tile_pool(name="keep", bufs=1))
+        all_codes = ctx.enter_context(tc.tile_pool(name="all_codes", bufs=TILES))
         stage = ctx.enter_context(tc.tile_pool(name="stage", bufs=3))
         pair = ctx.enter_context(tc.tile_pool(name="pair", bufs=2))
         results = ctx.enter_context(tc.tile_pool(name="results", bufs=4))
-        acc_pool = ctx.enter_context(tc.psum_pool(name="acc_pool", bufs=6))
-        turn_pool = ctx.enter_context(tc.psum_pool(name="turn_pool", bufs=2))
+        banks = ctx.enter_context(tc.psum_pool(name="banks", bufs=8))
 
         loud = keep.tile([P, TILES, KL], BF16, name="loud", align_bytes=64)
         rest = keep.tile([P, TILES, KR], BF16, name="rest", align_bytes=64)
         mom = keep.tile([P, TILES, N], BF16, name="mom", align_bytes=64)
-        basis = keep.tile([P, 4, N], BF16, name="basis", align_bytes=64)
+        basis_a = keep.tile([P, 4, HALF], BF16, name="basis_a", align_bytes=64)
+        basis_b = keep.tile([P, 4, HALF], BF16, name="basis_b", align_bytes=64)
+        basis = [basis_a, basis_b]
         w_words = keep.tile([P, REST, 2 * N], U8, name="w_words", align_bytes=64)
         w_scales = keep.tile([P, REST, N], U8, name="w_scales", align_bytes=64)
         b_codes = keep.tile([P, N], U32, name="b_codes", align_bytes=64)
@@ -60,8 +62,8 @@ def tile_soap_rotated_step_s1_kernel(
 
         ctx.enter_context(tc.manual_schedule())
 
-        def load_basis(c0, c1):
-            nc.sync.dma_start(out=basis[:, :, c0:c1], in_=basis_rows[:, :, c0:c1])
+        def load_basis(half):
+            nc.sync.dma_start(out=basis[half][:], in_=basis_rows[:, :, half * HALF : (half + 1) * HALF])
 
         def load_loud(r0, r1):
             nc.sync.dma_start(out=loud[:, r0:r1, :], in_=loud_rows[:, r0:r1, :])
@@ -76,27 +78,29 @@ def tile_soap_rotated_step_s1_kernel(
         nc.scalar.activation(out=warm[:], in_=one[:], func=ACT.Abs_reciprocal_sqrt)
         nc.vector.memset(w_scales[:].rearrange("p g n -> p (g n)").bitcast(I32), 0)
 
-        load_basis(0, HALF)
-        load_loud(0, 2)
+        load_basis(0)
+        for r in range(4):
+            nc.scalar.dma_start(out=w_scales[r:P:32, :, :].bitcast(I32), in_=scales_i32[r])
+        load_loud(0, 4)
         load_rest(0, 2)
-        load_basis(HALF, N)
+        load_basis(1)
+        load_rest(2, 4)
         nc.sync.dma_start(out=w_words[:].bitcast(I32), in_=words_i32)
         load_moment(0, 1)
         load_moment(1, 2)
-        load_rest(2, 4)
-        load_loud(2, 8)
-        load_moment(2, 4)
         load_rest(4, 6)
+        load_loud(4, 8)
+        load_moment(2, 4)
+        load_rest(6, 8)
         load_moment(4, 6)
+        load_moment(6, 8)
 
         make_identity(nc, ident[:])
-        for r in range(4):
-            nc.gpsimd.dma_start(out=w_scales[r:P:32, :, :].bitcast(I32), in_=scales_i32[r])
 
         def interleave_basis(engine_copy, c):
-            cols = slice(c * BANK, (c + 1) * BANK)
-            b_grouped = stage.tile([P, BANK, 4], BF16, name="b_grouped", align_bytes=64)
-            engine_copy(out=b_grouped[:], in_=basis[:, :, cols].rearrange("p j n -> p n j"))
+            cols = slice((c % 2) * BANK, (c % 2 + 1) * BANK)
+            b_grouped = pair.tile([P, BANK, 4], BF16, name="b_grouped", align_bytes=64)
+            engine_copy(out=b_grouped[:], in_=basis[c // 2][:, :, cols].rearrange("p j n -> p n j"))
             return b_grouped
 
         def quantize_basis(c, b_grouped):
@@ -111,11 +115,11 @@ def tile_soap_rotated_step_s1_kernel(
         codes = {}
         scales = {}
 
+        turned = {}
+
         def turn(i, b):
-            if b == 0:
-                g_grouped = pair.tile([P, PASSES * P * 4], BF16, name="g_grouped", align_bytes=64)
-                grouped[i] = g_grouped
-            turned = turn_pool.tile([P, 2, 2, P], F32, name="turned")
+            bank = banks.tile([P, BANK], F32, name="bank")
+            turned[i, b] = bank
             loud_words = loud[:, i, :].bitcast(F32)
             rest_words = rest[:, i, :].bitcast(F32)
             for s in range(2):
@@ -125,15 +129,21 @@ def tile_soap_rotated_step_s1_kernel(
                         src = loud_words[:, u:256:2]
                     else:
                         src = rest_words[:, 256 * (g - 1) + u : 256 * g : 2]
-                    nc.tensor.transpose(turned[:, s, u, :], src, ident[:])
+                    q = 2 * s + u
+                    nc.tensor.transpose(bank[:, q * P : (q + 1) * P], src, ident[:])
+
+        def interleave(i, b):
+            if b == 0:
+                g_grouped = stage.tile([P, PASSES * P * 4], BF16, name="g_grouped", align_bytes=64)
+                grouped[i] = g_grouped
             nc.scalar.copy(
                 out=grouped[i][:, 1024 * b : 1024 * (b + 1)].bitcast(F32).rearrange("p (s r u) -> p s r u", s=2, u=2),
-                in_=turned[:].rearrange("p s u r -> p s r u"),
+                in_=turned[i, b][:].rearrange("p (s u r) -> p s r u", s=2, u=2),
             )
 
         def quantize_tile(i):
-            g_codes = stage.tile([P, PASSES * P], U32, name="g_codes", align_bytes=64)
-            g_scales = stage.tile([P, PASSES * P], U8, name="g_scales", align_bytes=64)
+            g_codes = all_codes.tile([P, PASSES * P], U32, name="g_codes", align_bytes=64)
+            g_scales = all_codes.tile([P, PASSES * P], U8, name="g_scales", align_bytes=64)
             codes[i] = g_codes
             scales[i] = g_scales
             nc.vector.quantize_mx(out=g_codes[:].bitcast(E4M3X4), scales=g_scales[:], in_=grouped[i][:])
@@ -144,104 +154,109 @@ def tile_soap_rotated_step_s1_kernel(
         nm = {}
         st = {}
 
-        def multiply(h):
-            i = h // 2
-            acc[h] = []
-            for b in range(2):
-                n0 = (h % 2) * HALF + b * BANK
-                bank = acc_pool.tile([P, BANK], F32, name="bank")
-                acc[h].append(bank)
-                for g in range(PASSES):
-                    k_cols = slice(g * P, (g + 1) * P)
-                    if g == 0:
-                        rhs = b_codes[:, n0 : n0 + BANK].bitcast(E4M3X4)
-                        rhs_scale = b_scales[:, n0 : n0 + BANK]
-                    else:
-                        rhs = w_words[:, g - 1, 2 * n0 : 2 * (n0 + BANK)].bitcast(E2M1X4)
-                        rhs_scale = w_scales[:, g - 1, n0 : n0 + BANK]
-                    nc.tensor.matmul_mx(
-                        out=bank[:],
-                        lhsT=codes[i][:, k_cols].bitcast(E4M3X4),
-                        lhsT_scale=scales[i][:, k_cols],
-                        rhs=rhs,
-                        rhs_scale=rhs_scale,
-                        start=(g == 0),
-                        stop=(g == PASSES - 1),
-                    )
-
-        def square(h):
-            squares = stage.tile([P, HALF], F32, name="squares")
-            sq[h] = squares
-            for b in range(2):
-                nc.scalar.activation(
-                    out=squares[:, b * BANK : (b + 1) * BANK],
-                    in_=acc[h][b][:],
-                    func=ACT.Square,
-                    scale=(1 - BETA2) ** 0.5,
+        def multiply(j):
+            i = j // 4
+            n0 = (j % 4) * BANK
+            bank = banks.tile([P, BANK], F32, name="bank")
+            acc[j] = bank
+            for g in range(PASSES):
+                k_cols = slice(g * P, (g + 1) * P)
+                if g == 0:
+                    rhs = b_codes[:, n0 : n0 + BANK].bitcast(E4M3X4)
+                    rhs_scale = b_scales[:, n0 : n0 + BANK]
+                else:
+                    rhs = w_words[:, g - 1, 2 * n0 : 2 * (n0 + BANK)].bitcast(E2M1X4)
+                    rhs_scale = w_scales[:, g - 1, n0 : n0 + BANK]
+                nc.tensor.matmul_mx(
+                    out=bank[:],
+                    lhsT=codes[i][:, k_cols].bitcast(E4M3X4),
+                    lhsT_scale=scales[i][:, k_cols],
+                    rhs=rhs,
+                    rhs_scale=rhs_scale,
+                    start=(g == 0),
+                    stop=(g == PASSES - 1),
                 )
 
-        def update_moment(h):
-            i = h // 2
-            if h % 2 == 0:
+        def square(j):
+            squares = stage.tile([P, BANK], F32, name="squares")
+            sq[j] = squares
+            nc.scalar.activation(out=squares[:], in_=acc[j][:], func=ACT.Square, scale=(1 - BETA2) ** 0.5)
+
+        def store(rows, tile, i, j):
+            if i == TILES - 1:
+                if j % 2 == 1:
+                    cols = slice((j % 4 - 1) * BANK, (j % 4 + 1) * BANK)
+                    nc.sync.dma_start(out=rows[:, i, cols], in_=tile[:, cols])
+            elif j % 4 == 3:
+                nc.sync.dma_start(out=rows[:, i, :], in_=tile[:])
+
+        def update_moment(j):
+            i = j // 4
+            if j % 4 == 0:
                 nm_tile = results.tile([P, N], F32, name="nm_tile")
                 nm[i] = nm_tile
-            cols = slice((h % 2) * HALF, (h % 2 + 1) * HALF)
+            cols = slice((j % 4) * BANK, (j % 4 + 1) * BANK)
             nc.vector.scalar_tensor_tensor(
-                out=nm[i][:, cols], in0=mom[:, i, cols], scalar=BETA2, in1=sq[h][:], op0=ALU.mult, op1=ALU.add
+                out=nm[i][:, cols], in0=mom[:, i, cols], scalar=BETA2, in1=sq[j][:], op0=ALU.mult, op1=ALU.add
             )
-            if h % 2 == 1:
-                nc.sync.dma_start(out=new_moment_rows[:, i, :], in_=nm[i][:])
+            store(new_moment_rows, nm[i], i, j)
 
-        def root(h):
-            i = h // 2
-            cols = slice((h % 2) * HALF, (h % 2 + 1) * HALF)
-            roots = pair.tile([P, HALF], F32, name="roots")
-            rs[h] = roots
+        def root(j):
+            i = j // 4
+            cols = slice((j % 4) * BANK, (j % 4 + 1) * BANK)
+            roots = stage.tile([P, BANK], F32, name="roots")
+            rs[j] = roots
             nc.scalar.activation(out=roots[:], in_=nm[i][:, cols], func=ACT.Abs_reciprocal_sqrt)
 
-        def normalise(h):
-            i = h // 2
-            if h % 2 == 0:
+        def normalise(j):
+            i = j // 4
+            if j % 4 == 0:
                 st_tile = results.tile([P, N], F32, name="st_tile")
                 st[i] = st_tile
-            for b in range(2):
-                n0 = (h % 2) * HALF + b * BANK
-                nc.vector.tensor_tensor(
-                    out=st[i][:, n0 : n0 + BANK], in0=acc[h][b][:], in1=rs[h][:, b * BANK : (b + 1) * BANK], op=ALU.mult
-                )
-            if h % 2 == 1:
-                nc.sync.dma_start(out=step_rows[:, i, :], in_=st[i][:])
-                if i == 0:
-                    load_rest(6, 8)
-                if i == 1:
-                    load_moment(6, 8)
+            cols = slice((j % 4) * BANK, (j % 4 + 1) * BANK)
+            nc.vector.tensor_tensor(out=st[i][:, cols], in0=acc[j][:], in1=rs[j][:], op=ALU.mult)
+            store(step_rows, st[i], i, j)
 
         b0 = interleave_basis(nc.vector.tensor_copy, 0)
         b1 = interleave_basis(nc.scalar.copy, 1)
-        turn(0, 0)
-        turn(0, 1)
         quantize_basis(0, b0)
-        turn(1, 0)
-        turn(1, 1)
         quantize_basis(1, b1)
+        for i in range(2):
+            for b in range(2):
+                turn(i, b)
+            for b in range(2):
+                interleave(i, b)
         quantize_tile(0)
         b2 = interleave_basis(nc.vector.tensor_copy, 2)
         b3 = interleave_basis(nc.scalar.copy, 3)
         quantize_tile(1)
         quantize_basis(2, b2)
+        for i in range(2, 4):
+            for b in range(2):
+                turn(i, b)
+            for b in range(2):
+                interleave(i, b)
         quantize_basis(3, b3)
+        quantize_tile(2)
+        quantize_tile(3)
 
-        for h in range(2 * TILES):
-            i = h // 2
-            multiply(h)
-            square(h)
-            update_moment(h)
-            if h > 0:
-                root(h - 1)
-                normalise(h - 1)
-            if i + 2 < TILES:
-                turn(i + 2, h % 2)
-                if h % 2 == 1:
-                    quantize_tile(i + 2)
-        root(2 * TILES - 1)
-        normalise(2 * TILES - 1)
+        units = 4 * TILES
+        for j in range(units + 3):
+            i = j // 4
+            if j < units:
+                multiply(j)
+                if j % 4 == 0 and i + 4 < TILES:
+                    turn(i + 4, 0)
+                    turn(i + 4, 1)
+                square(j)
+            if 1 <= j < units + 1:
+                update_moment(j - 1)
+            if 2 <= j < units + 2:
+                root(j - 2)
+            if 3 <= j:
+                normalise(j - 3)
+            if i + 4 < TILES:
+                if j % 4 in (1, 2):
+                    interleave(i + 4, j % 4 - 1)
+                if j % 4 == 3:
+                    quantize_tile(i + 4)

@@ -81,19 +81,17 @@ def tile_soap_rotated_step_s1_kernel(
         load_basis(0)
         for r in range(4):
             nc.scalar.dma_start(out=w_scales[r:P:32, :, :].bitcast(I32), in_=scales_i32[r])
-        load_loud(0, 4)
         load_rest(0, 2)
+        load_loud(0, 4)
         load_basis(1)
-        load_rest(2, 4)
         nc.sync.dma_start(out=w_words[:].bitcast(I32), in_=words_i32)
         load_moment(0, 1)
+        load_rest(2, 4)
         load_moment(1, 2)
-        load_rest(4, 6)
+        load_rest(4, 8)
         load_loud(4, 8)
         load_moment(2, 4)
-        load_rest(6, 8)
-        load_moment(4, 6)
-        load_moment(6, 8)
+        load_moment(4, 8)
 
         make_identity(nc, ident[:])
 
@@ -184,8 +182,9 @@ def tile_soap_rotated_step_s1_kernel(
 
         def store(rows, tile, i, j):
             if i == TILES - 1:
-                if j % 2 == 1:
-                    cols = slice((j % 4 - 1) * BANK, (j % 4 + 1) * BANK)
+                first = {1: 0, 2: 2, 3: 3}.get(j % 4)
+                if first is not None:
+                    cols = slice(first * BANK, (j % 4 + 1) * BANK)
                     nc.sync.dma_start(out=rows[:, i, cols], in_=tile[:, cols])
             elif j % 4 == 3:
                 nc.sync.dma_start(out=rows[:, i, :], in_=tile[:])
@@ -217,37 +216,29 @@ def tile_soap_rotated_step_s1_kernel(
             nc.vector.tensor_tensor(out=st[i][:, cols], in0=acc[j][:], in1=rs[j][:], op=ALU.mult)
             store(step_rows, st[i], i, j)
 
+        def prepare(i):
+            for b in range(2):
+                turn(i, b)
+            for b in range(2):
+                interleave(i, b)
+
         b0 = interleave_basis(nc.vector.tensor_copy, 0)
-        b1 = interleave_basis(nc.scalar.copy, 1)
+        b1 = interleave_basis(nc.vector.tensor_copy, 1)
         quantize_basis(0, b0)
         quantize_basis(1, b1)
-        for i in range(2):
-            for b in range(2):
-                turn(i, b)
-            for b in range(2):
-                interleave(i, b)
+        prepare(0)
         quantize_tile(0)
+        prepare(1)
         b2 = interleave_basis(nc.vector.tensor_copy, 2)
-        b3 = interleave_basis(nc.scalar.copy, 3)
+        b3 = interleave_basis(nc.vector.tensor_copy, 3)
         quantize_tile(1)
         quantize_basis(2, b2)
-        for i in range(2, 4):
-            for b in range(2):
-                turn(i, b)
-            for b in range(2):
-                interleave(i, b)
         quantize_basis(3, b3)
-        quantize_tile(2)
-        quantize_tile(3)
 
         units = 4 * TILES
         for j in range(units + 3):
-            i = j // 4
             if j < units:
                 multiply(j)
-                if j % 4 == 0 and i + 4 < TILES:
-                    turn(i + 4, 0)
-                    turn(i + 4, 1)
                 square(j)
             if 1 <= j < units + 1:
                 update_moment(j - 1)
@@ -255,8 +246,13 @@ def tile_soap_rotated_step_s1_kernel(
                 root(j - 2)
             if 3 <= j:
                 normalise(j - 3)
-            if i + 4 < TILES:
-                if j % 4 in (1, 2):
-                    interleave(i + 4, j % 4 - 1)
-                if j % 4 == 3:
-                    quantize_tile(i + 4)
+            m, phase = divmod(j + 2, 4)
+            if phase == 0 and m + 1 < TILES:
+                turn(m + 1, 0)
+                turn(m + 1, 1)
+            if phase == 1 and m + 1 < TILES:
+                interleave(m + 1, 0)
+            if phase == 2 and 1 < m + 1 < TILES:
+                interleave(m + 1, 1)
+            if phase == 3 and 1 < m + 1 < TILES:
+                quantize_tile(m + 1)

@@ -52,7 +52,9 @@ def tile_soap_rotated_step_s1_kernel(
         basis_a = keep.tile([P, 4, HALF], BF16, name="basis_a", align_bytes=64)
         basis_b = keep.tile([P, 4, HALF], BF16, name="basis_b", align_bytes=64)
         basis = [basis_a, basis_b]
-        w_words = keep.tile([P, REST, 2 * N], U8, name="w_words", align_bytes=64)
+        words_a = keep.tile([P, REST, 2 * HALF], U8, name="words_a", align_bytes=64)
+        words_b = keep.tile([P, REST, 2 * HALF], U8, name="words_b", align_bytes=64)
+        words = [words_a, words_b]
         w_scales = keep.tile([P, REST, N], U8, name="w_scales", align_bytes=64)
         b_codes = keep.tile([P, N], U32, name="b_codes", align_bytes=64)
         b_scales = keep.tile([P, N], U8, name="b_scales", align_bytes=64)
@@ -71,6 +73,10 @@ def tile_soap_rotated_step_s1_kernel(
         def load_rest(r0, r1):
             nc.sync.dma_start(out=rest[:, r0:r1, :], in_=rest_rows[:, r0:r1, :])
 
+        def load_words(half):
+            cols = slice(half * HALF // 2, (half + 1) * HALF // 2)
+            nc.sync.dma_start(out=words[half][:].bitcast(I32), in_=words_i32[:, :, cols])
+
         def load_moment(r0, r1):
             nc.sync.dma_start(out=mom[:, r0:r1, :], in_=moment_rows[:, r0:r1, :])
 
@@ -83,30 +89,34 @@ def tile_soap_rotated_step_s1_kernel(
             nc.scalar.dma_start(out=w_scales[r:P:32, :, :].bitcast(I32), in_=scales_i32[r])
         load_rest(0, 2)
         load_loud(0, 4)
+        load_words(0)
         load_basis(1)
-        nc.sync.dma_start(out=w_words[:].bitcast(I32), in_=words_i32)
         load_moment(0, 1)
         load_rest(2, 4)
         load_moment(1, 2)
-        load_rest(4, 8)
+        load_words(1)
         load_loud(4, 8)
+        load_rest(4, 8)
         load_moment(2, 4)
         load_moment(4, 8)
 
         make_identity(nc, ident[:])
 
-        def interleave_basis(engine_copy, c):
-            cols = slice((c % 2) * BANK, (c % 2 + 1) * BANK)
-            b_grouped = pair.tile([P, BANK, 4], BF16, name="b_grouped", align_bytes=64)
-            engine_copy(out=b_grouped[:], in_=basis[c // 2][:, :, cols].rearrange("p j n -> p n j"))
-            return b_grouped
+        grouped_basis = {}
 
-        def quantize_basis(c, b_grouped):
+        def interleave_basis(engine_copy, c, n0=0, n1=BANK):
+            if n0 == 0:
+                b_grouped = pair.tile([P, BANK, 4], BF16, name="b_grouped", align_bytes=64)
+                grouped_basis[c] = b_grouped
+            cols = slice((c % 2) * BANK + n0, (c % 2) * BANK + n1)
+            engine_copy(out=grouped_basis[c][:, n0:n1, :], in_=basis[c // 2][:, :, cols].rearrange("p j n -> p n j"))
+
+        def quantize_basis(c):
             cols = slice(c * BANK, (c + 1) * BANK)
             nc.vector.quantize_mx(
                 out=b_codes[:, cols].bitcast(E4M3X4),
                 scales=b_scales[:, cols],
-                in_=b_grouped[:].rearrange("p n j -> p (n j)"),
+                in_=grouped_basis[c][:].rearrange("p n j -> p (n j)"),
             )
 
         grouped = {}
@@ -153,8 +163,9 @@ def tile_soap_rotated_step_s1_kernel(
         st = {}
 
         def multiply(j):
-            i = j // 4
-            n0 = (j % 4) * BANK
+            i, c = order[j]
+            n0 = c * BANK
+            w0 = 2 * (n0 % HALF)
             bank = banks.tile([P, BANK], F32, name="bank")
             acc[j] = bank
             for g in range(PASSES):
@@ -163,7 +174,7 @@ def tile_soap_rotated_step_s1_kernel(
                     rhs = b_codes[:, n0 : n0 + BANK].bitcast(E4M3X4)
                     rhs_scale = b_scales[:, n0 : n0 + BANK]
                 else:
-                    rhs = w_words[:, g - 1, 2 * n0 : 2 * (n0 + BANK)].bitcast(E2M1X4)
+                    rhs = words[c // 2][:, g - 1, w0 : w0 + 2 * BANK].bitcast(E2M1X4)
                     rhs_scale = w_scales[:, g - 1, n0 : n0 + BANK]
                 nc.tensor.matmul_mx(
                     out=bank[:],
@@ -180,41 +191,42 @@ def tile_soap_rotated_step_s1_kernel(
             sq[j] = squares
             nc.scalar.activation(out=squares[:], in_=acc[j][:], func=ACT.Square, scale=(1 - BETA2) ** 0.5)
 
-        def store(rows, tile, i, j):
+        def store(rows, tile, i, c):
             if i == TILES - 1:
-                first = {1: 0, 2: 2, 3: 3}.get(j % 4)
+                first = {1: 0, 2: 2, 3: 3}.get(c)
                 if first is not None:
-                    cols = slice(first * BANK, (j % 4 + 1) * BANK)
+                    cols = slice(first * BANK, (c + 1) * BANK)
                     nc.sync.dma_start(out=rows[:, i, cols], in_=tile[:, cols])
-            elif j % 4 == 3:
+            elif c == 3:
                 nc.sync.dma_start(out=rows[:, i, :], in_=tile[:])
 
         def update_moment(j):
-            i = j // 4
-            if j % 4 == 0:
+            i, c = order[j]
+            if c == 0:
                 nm_tile = results.tile([P, N], F32, name="nm_tile")
                 nm[i] = nm_tile
-            cols = slice((j % 4) * BANK, (j % 4 + 1) * BANK)
+            cols = slice(c * BANK, (c + 1) * BANK)
             nc.vector.scalar_tensor_tensor(
                 out=nm[i][:, cols], in0=mom[:, i, cols], scalar=BETA2, in1=sq[j][:], op0=ALU.mult, op1=ALU.add
             )
-            store(new_moment_rows, nm[i], i, j)
+            store(new_moment_rows, nm[i], i, c)
 
         def root(j):
-            i = j // 4
-            cols = slice((j % 4) * BANK, (j % 4 + 1) * BANK)
+            i, c = order[j]
             roots = stage.tile([P, BANK], F32, name="roots")
             rs[j] = roots
-            nc.scalar.activation(out=roots[:], in_=nm[i][:, cols], func=ACT.Abs_reciprocal_sqrt)
+            nc.scalar.activation(
+                out=roots[:], in_=nm[i][:, c * BANK : (c + 1) * BANK], func=ACT.Abs_reciprocal_sqrt
+            )
 
         def normalise(j):
-            i = j // 4
-            if j % 4 == 0:
+            i, c = order[j]
+            if c == 0:
                 st_tile = results.tile([P, N], F32, name="st_tile")
                 st[i] = st_tile
-            cols = slice((j % 4) * BANK, (j % 4 + 1) * BANK)
+            cols = slice(c * BANK, (c + 1) * BANK)
             nc.vector.tensor_tensor(out=st[i][:, cols], in0=acc[j][:], in1=rs[j][:], op=ALU.mult)
-            store(step_rows, st[i], i, j)
+            store(step_rows, st[i], i, c)
 
         def prepare(i):
             for b in range(2):
@@ -222,20 +234,42 @@ def tile_soap_rotated_step_s1_kernel(
             for b in range(2):
                 interleave(i, b)
 
-        b0 = interleave_basis(nc.vector.tensor_copy, 0)
-        b1 = interleave_basis(nc.vector.tensor_copy, 1)
-        quantize_basis(0, b0)
-        quantize_basis(1, b1)
+        interleave_basis(nc.vector.tensor_copy, 0)
+        interleave_basis(nc.vector.tensor_copy, 1)
+        quantize_basis(0)
+        quantize_basis(1)
         prepare(0)
         quantize_tile(0)
         prepare(1)
-        b2 = interleave_basis(nc.vector.tensor_copy, 2)
-        b3 = interleave_basis(nc.vector.tensor_copy, 3)
         quantize_tile(1)
-        quantize_basis(2, b2)
-        quantize_basis(3, b3)
 
-        units = 4 * TILES
+        order = [(i, 2 * half + c) for half in range(2) for i in range(2) for c in range(2)]
+        order += [(i, c) for i in range(2, TILES) for c in range(4)]
+        units = len(order)
+        later = {}
+
+        def at(j, call, *args):
+            later.setdefault(j, []).append((call, args))
+
+        at(0, interleave_basis, nc.vector.tensor_copy, 2)
+        at(1, interleave_basis, nc.vector.tensor_copy, 3)
+        at(2, quantize_basis, 2)
+        at(2, quantize_basis, 3)
+        for i in (2, 3):
+            for b in range(2):
+                at(3, turn, i, b)
+        at(3, interleave, 2, 0)
+        at(3, interleave, 2, 1)
+        at(4, quantize_tile, 2)
+        at(4, interleave, 3, 0)
+        at(6, interleave, 3, 1)
+        at(7, quantize_tile, 3)
+        for i in range(4, TILES):
+            at(4 * i - 5, turn, i, 0)
+            at(4 * i - 5, turn, i, 1)
+            at(4 * i - 4, interleave, i, 0)
+            at(4 * i - 3, interleave, i, 1)
+            at(4 * i - 2, quantize_tile, i)
         for j in range(units + 3):
             if j < units:
                 multiply(j)
@@ -246,13 +280,5 @@ def tile_soap_rotated_step_s1_kernel(
                 root(j - 2)
             if 3 <= j:
                 normalise(j - 3)
-            m, phase = divmod(j + 2, 4)
-            if phase == 0 and m + 1 < TILES:
-                turn(m + 1, 0)
-                turn(m + 1, 1)
-            if phase == 1 and m + 1 < TILES:
-                interleave(m + 1, 0)
-            if phase == 2 and 1 < m + 1 < TILES:
-                interleave(m + 1, 1)
-            if phase == 3 and 1 < m + 1 < TILES:
-                quantize_tile(m + 1)
+            for call, args in later.get(j, []):
+                call(*args)

from contextlib import ExitStack

import concourse.mybir as mybir
from concourse.masks import make_identity

M, KL, KR, N = 1024, 512, 1536, 2048
BETA2 = 0.9
FLOPS = 2 * M * (KL + KR) * N

F32 = mybir.dt.float32
BF16 = mybir.dt.bfloat16
I32 = mybir.dt.int32
U32 = mybir.dt.uint32
U8 = mybir.dt.uint8
E4M3X4 = mybir.dt.float8_e4m3fn_x4
E2M1X4 = mybir.dt.float4_e2m1fn_x4
ACT = mybir.ActivationFunctionType
ALU = mybir.AluOpType

P = 128
TILES = M // P
BANK = 512
HALF = 2 * BANK
PASSES = 4
REST = KR // 512


def tile_soap_rotated_step_s1_kernel(
    tc, grad_loud, grad_rest, basis_loud, basis_rest_words, basis_rest_scales, moment, out_0, out_1
):
    nc = tc.nc
    loud_rows = grad_loud.rearrange("(p r) k -> p r k", r=TILES)
    rest_rows = grad_rest.rearrange("(p r) k -> p r k", r=TILES)
    moment_rows = moment.rearrange("(p r) n -> p r n", r=TILES)
    step_rows = out_0.rearrange("(p r) n -> p r n", r=TILES)
    new_moment_rows = out_1.rearrange("(p r) n -> p r n", r=TILES)
    basis_rows = basis_loud.rearrange("(p j) n -> p j n", j=4)
    words_i32 = basis_rest_words.bitcast(I32).rearrange("g p w -> p g w")
    scales_i32 = basis_rest_scales.bitcast(I32).rearrange("g (q r) w -> r q g w", r=4)

    with ExitStack() as ctx:
        keep = ctx.enter_context(tc.tile_pool(name="keep", bufs=1))
        all_codes = ctx.enter_context(tc.tile_pool(name="all_codes", bufs=TILES))
        stage = ctx.enter_context(tc.tile_pool(name="stage", bufs=3))
        pair = ctx.enter_context(tc.tile_pool(name="pair", bufs=2))
        results = ctx.enter_context(tc.tile_pool(name="results", bufs=4))
        banks = ctx.enter_context(tc.psum_pool(name="banks", bufs=8))

        loud = keep.tile([P, TILES, KL], BF16, name="loud", align_bytes=64)
        rest = keep.tile([P, TILES, KR], BF16, name="rest", align_bytes=64)
        mom = keep.tile([P, TILES, N], BF16, name="mom", align_bytes=64)
        basis_a = keep.tile([P, 4, HALF], BF16, name="basis_a", align_bytes=64)
        basis_b = keep.tile([P, 4, HALF], BF16, name="basis_b", align_bytes=64)
        basis = [basis_a, basis_b]
        words_a = keep.tile([P, REST, 2 * HALF], U8, name="words_a", align_bytes=64)
        words_b = keep.tile([P, REST, 2 * HALF], U8, name="words_b", align_bytes=64)
        words = [words_a, words_b]
        w_scales = keep.tile([P, REST, N], U8, name="w_scales", align_bytes=64)
        b_codes = keep.tile([P, N], U32, name="b_codes", align_bytes=64)
        b_scales = keep.tile([P, N], U8, name="b_scales", align_bytes=64)
        ident = keep.tile([P, P], F32, name="ident", align_bytes=64)
        one = keep.tile([P, 1], F32, name="one")
        warm = keep.tile([P, 1], F32, name="warm")

        ctx.enter_context(tc.manual_schedule())

        def load_basis(half):
            nc.sync.dma_start(out=basis[half][:], in_=basis_rows[:, :, half * HALF : (half + 1) * HALF])

        def load_loud(r0, r1):
            nc.sync.dma_start(out=loud[:, r0:r1, :], in_=loud_rows[:, r0:r1, :])

        def load_rest(r0, r1):
            nc.sync.dma_start(out=rest[:, r0:r1, :], in_=rest_rows[:, r0:r1, :])

        def load_words(half):
            cols = slice(half * HALF // 2, (half + 1) * HALF // 2)
            nc.sync.dma_start(out=words[half][:].bitcast(I32), in_=words_i32[:, :, cols])

        def load_moment(r0, r1):
            nc.sync.dma_start(out=mom[:, r0:r1, :], in_=moment_rows[:, r0:r1, :])

        nc.gpsimd.memset(one[:], 1.0)
        nc.scalar.activation(out=warm[:], in_=one[:], func=ACT.Abs_reciprocal_sqrt)
        nc.vector.memset(w_scales[:].rearrange("p g n -> p (g n)").bitcast(I32), 0)

        load_basis(0)
        for r in range(4):
            nc.scalar.dma_start(out=w_scales[r:P:32, :, :].bitcast(I32), in_=scales_i32[r])
        load_rest(0, 2)
        load_loud(0, 4)
        load_words(0)
        load_basis(1)
        load_moment(0, 1)
        load_rest(2, 4)
        load_moment(1, 2)
        load_words(1)
        load_loud(4, 8)
        load_rest(4, 8)
        load_moment(2, 4)
        load_moment(4, 8)

        make_identity(nc, ident[:])

        grouped_basis = {}

        def interleave_basis(engine_copy, c, n0=0, n1=BANK):
            if n0 == 0:
                b_grouped = pair.tile([P, BANK, 4], BF16, name="b_grouped", align_bytes=64)
                grouped_basis[c] = b_grouped
            cols = slice((c % 2) * BANK + n0, (c % 2) * BANK + n1)
            engine_copy(out=grouped_basis[c][:, n0:n1, :], in_=basis[c // 2][:, :, cols].rearrange("p j n -> p n j"))

        def quantize_basis(c):
            cols = slice(c * BANK, (c + 1) * BANK)
            nc.vector.quantize_mx(
                out=b_codes[:, cols].bitcast(E4M3X4),
                scales=b_scales[:, cols],
                in_=grouped_basis[c][:].rearrange("p n j -> p (n j)"),
            )

        grouped = {}
        codes = {}
        scales = {}

        turned = {}

        def turn(i, b):
            bank = banks.tile([P, BANK], F32, name="bank")
            turned[i, b] = bank
            loud_words = loud[:, i, :].bitcast(F32)
            rest_words = rest[:, i, :].bitcast(F32)
            for s in range(2):
                g = 2 * b + s
                for u in range(2):
                    if g == 0:
                        src = loud_words[:, u:256:2]
                    else:
                        src = rest_words[:, 256 * (g - 1) + u : 256 * g : 2]
                    q = 2 * s + u
                    nc.tensor.transpose(bank[:, q * P : (q + 1) * P], src, ident[:])

        def interleave(i, b):
            if b == 0:
                g_grouped = stage.tile([P, PASSES * P * 4], BF16, name="g_grouped", align_bytes=64)
                grouped[i] = g_grouped
            nc.scalar.copy(
                out=grouped[i][:, 1024 * b : 1024 * (b + 1)].bitcast(F32).rearrange("p (s r u) -> p s r u", s=2, u=2),
                in_=turned[i, b][:].rearrange("p (s u r) -> p s r u", s=2, u=2),
            )

        def quantize_tile(i):
            g_codes = all_codes.tile([P, PASSES * P], U32, name="g_codes", align_bytes=64)
            g_scales = all_codes.tile([P, PASSES * P], U8, name="g_scales", align_bytes=64)
            codes[i] = g_codes
            scales[i] = g_scales
            nc.vector.quantize_mx(out=g_codes[:].bitcast(E4M3X4), scales=g_scales[:], in_=grouped[i][:])

        acc = {}
        sq = {}
        rs = {}
        nm = {}
        st = {}

        def multiply(j):
            i, c = order[j]
            n0 = c * BANK
            w0 = 2 * (n0 % HALF)
            bank = banks.tile([P, BANK], F32, name="bank")
            acc[j] = bank
            for g in range(PASSES):
                k_cols = slice(g * P, (g + 1) * P)
                if g == 0:
                    rhs = b_codes[:, n0 : n0 + BANK].bitcast(E4M3X4)
                    rhs_scale = b_scales[:, n0 : n0 + BANK]
                else:
                    rhs = words[c // 2][:, g - 1, w0 : w0 + 2 * BANK].bitcast(E2M1X4)
                    rhs_scale = w_scales[:, g - 1, n0 : n0 + BANK]
                nc.tensor.matmul_mx(
                    out=bank[:],
                    lhsT=codes[i][:, k_cols].bitcast(E4M3X4),
                    lhsT_scale=scales[i][:, k_cols],
                    rhs=rhs,
                    rhs_scale=rhs_scale,
                    start=(g == 0),
                    stop=(g == PASSES - 1),
                )

        def square(j):
            squares = stage.tile([P, BANK], F32, name="squares")
            sq[j] = squares
            nc.scalar.activation(out=squares[:], in_=acc[j][:], func=ACT.Square, scale=(1 - BETA2) ** 0.5)

        def store(rows, tile, i, c):
            if i == TILES - 1:
                first = {1: 0, 2: 2, 3: 3}.get(c)
                if first is not None:
                    cols = slice(first * BANK, (c + 1) * BANK)
                    nc.sync.dma_start(out=rows[:, i, cols], in_=tile[:, cols])
            elif c == 3:
                nc.sync.dma_start(out=rows[:, i, :], in_=tile[:])

        def update_moment(j):
            i, c = order[j]
            if c == 0:
                nm_tile = results.tile([P, N], F32, name="nm_tile")
                nm[i] = nm_tile
            cols = slice(c * BANK, (c + 1) * BANK)
            nc.vector.scalar_tensor_tensor(
                out=nm[i][:, cols], in0=mom[:, i, cols], scalar=BETA2, in1=sq[j][:], op0=ALU.mult, op1=ALU.add
            )
            store(new_moment_rows, nm[i], i, c)

        def root(j):
            i, c = order[j]
            roots = stage.tile([P, BANK], F32, name="roots")
            rs[j] = roots
            nc.scalar.activation(
                out=roots[:], in_=nm[i][:, c * BANK : (c + 1) * BANK], func=ACT.Abs_reciprocal_sqrt
            )

        def normalise(j):
            i, c = order[j]
            if c == 0:
                st_tile = results.tile([P, N], F32, name="st_tile")
                st[i] = st_tile
            cols = slice(c * BANK, (c + 1) * BANK)
            nc.vector.tensor_tensor(out=st[i][:, cols], in0=acc[j][:], in1=rs[j][:], op=ALU.mult)
            store(step_rows, st[i], i, c)

        def prepare(i):
            for b in range(2):
                turn(i, b)
            for b in range(2):
                interleave(i, b)

        interleave_basis(nc.vector.tensor_copy, 0)
        interleave_basis(nc.vector.tensor_copy, 1)
        quantize_basis(0)
        quantize_basis(1)
        prepare(0)
        quantize_tile(0)
        prepare(1)
        quantize_tile(1)

        order = [(i, 2 * half + c) for half in range(2) for i in range(2) for c in range(2)]
        order += [(i, c) for i in range(2, TILES) for c in range(4)]
        units = len(order)
        later = {}

        def at(j, call, *args):
            later.setdefault(j, []).append((call, args))

        at(0, interleave_basis, nc.vector.tensor_copy, 2)
        at(1, interleave_basis, nc.vector.tensor_copy, 3)
        at(2, quantize_basis, 2)
        at(2, quantize_basis, 3)
        for i in (2, 3):
            for b in range(2):
                at(3, turn, i, b)
        at(3, interleave, 2, 0)
        at(3, interleave, 2, 1)
        at(4, quantize_tile, 2)
        at(4, interleave, 3, 0)
        at(6, interleave, 3, 1)
        at(7, quantize_tile, 3)
        for i in range(4, TILES):
            at(4 * i - 5, turn, i, 0)
            at(4 * i - 5, turn, i, 1)
            at(4 * i - 4, interleave, i, 0)
            at(4 * i - 3, interleave, i, 1)
            at(4 * i - 2, quantize_tile, i)
        for j in range(units + 3):
            if j < units:
                multiply(j)
                square(j)
            if 1 <= j < units + 1:
                update_moment(j - 1)
            if 2 <= j < units + 2:
                root(j - 2)
            if 3 <= j:
                normalise(j - 3)
            for call, args in later.get(j, []):
                call(*args)
